import numpy as np
import ml_dtypes


def mxq(x, axis, fmt="e4m3"):
    dtype, down = {"e4m3": (ml_dtypes.float8_e4m3fn, 7), "e5m2": (ml_dtypes.float8_e5m2, 14)}[fmt]
    v = np.moveaxis(np.asarray(x, np.float32).astype(ml_dtypes.bfloat16).astype(np.float64), axis, -1)
    blocks = v.reshape(v.shape[:-1] + (-1, 32))
    amax = np.abs(blocks).max(-1, keepdims=True)
    byte = np.maximum(np.where(amax > 0, np.frexp(amax)[1] - 1 + 127, 0) - down, 1)
    scale = np.exp2(byte - 127.0)
    codes = (blocks / scale).astype(np.float32).astype(dtype).astype(np.float64)
    return np.moveaxis((codes * scale).reshape(v.shape), -1, axis)


WIDE = False


def mx_kscale(k):
    if not WIDE:
        return np.ones(k)
    levels = np.array([10, -10, 5, -5, 0])
    if k % 512:
        return np.exp2(np.random.permutation(np.resize(levels, k // 32))).repeat(32)
    a = np.empty((k // 512, 16))
    for p in range(k // 512):
        a[p, :8] = np.random.permutation(np.resize(levels, 8))
        for g in range(8):
            far = levels[np.abs(levels - a[p, g]) >= 10]
            a[p, g + 8] = far[np.random.randint(len(far))]
    return np.exp2(a.ravel()).repeat(32)


def f64(x):
    return np.asarray(x).astype(np.float64)


def striped(idx):
    return np.tile(idx.reshape(-1, 16).T, (8, 1)).astype(np.uint16)


def unstriped(offs):
    return offs[:16].T.reshape(-1).astype(np.int64)


def pack_weight(w):
    k, n = w.shape
    w = f64(np.asarray(w, np.float32).astype(ml_dtypes.bfloat16)).reshape(k // 32, 32, n)
    amax = np.abs(w).max(1)
    byte = np.clip(np.where(amax > 0, np.frexp(amax)[1] - 1 + 127 - 7, 1), 1, 254)
    scaled = (w * np.exp2(127.0 - byte)[:, None, :]).reshape(k, n).astype(np.float32)
    words = np.ascontiguousarray(scaled.reshape(k // 512, 128, 4, n).transpose(0, 1, 3, 2)).astype(ml_dtypes.float8_e4m3fn).view(np.uint8)
    return words, np.ascontiguousarray(byte.astype(np.uint8).reshape(k // 512, 16, n))


def unpack_weight(words, scales):
    g, p, n, _ = words.shape
    vals = np.ascontiguousarray(words).view(ml_dtypes.float8_e4m3fn).astype(np.float64) * np.repeat(np.exp2(scales.astype(np.float64) - 127.0), 8, axis=1)[..., None]
    return vals.transpose(0, 1, 3, 2).reshape(g * 512, n)


def sigmoid(v):
    return 1.0 / (1.0 + np.exp(-np.maximum(v, -700.0)))


K, T, S, W, N = 512, 2048, 512, 1024, 256


def setup_inputs():
    n = np.random.standard_normal
    s = mx_kscale(K)[:, None]
    packed_xT = pack_weight(n((K, T)) * s)
    packed_eT = pack_weight(n((K, W)) * s)
    return {
        "x_words": packed_xT[0],
        "x_scales": packed_xT[1],
        "e_words": packed_eT[0],
        "e_scales": packed_eT[1],
        "win": (n((K, N)) / np.sqrt(2 * K) / s).astype(np.float32),
        "vin": (n((K, N)) / np.sqrt(2 * K) / s).astype(np.float32),
        "wfo": (n((K, N)) / np.sqrt(2 * K) / s).astype(np.float32),
        "vfo": (n((K, N)) / np.sqrt(2 * K) / s).astype(np.float32),
        "wex": (n((K, N)) / np.sqrt(2 * K) / s).astype(np.float32),
        "vex": (n((K, N)) / np.sqrt(2 * K) / s).astype(np.float32),
        "wca": (n((K, N)) / np.sqrt(2 * K) / s).astype(np.float32),
        "vca": (n((K, N)) / np.sqrt(2 * K) / s).astype(np.float32),
        "cell": (n((N, T))).astype(np.float32),
        "offs": striped(np.random.permutation(T)[:S]),
        "tok": striped(np.random.permutation(W)[:S]),
    }


def reference(x_words, x_scales, e_words, e_scales, win, vin, wfo, vfo, wex, vex, wca, vca, cell, offs, tok):
    xq = unpack_weight(x_words, x_scales)[:, unstriped(offs)]
    e_tok = unpack_weight(e_words, e_scales)[:, unstriped(tok)]
    b = sigmoid(mxq(f64(wex), 0, "e4m3").T @ xq + mxq(f64(vex), 0, "e4m3").T @ e_tok)
    old = f64(cell)[:, unstriped(offs)]
    f = sigmoid(mxq(f64(wfo), 0, "e4m3").T @ xq + mxq(f64(vfo), 0, "e4m3").T @ e_tok)
    a = sigmoid(mxq(f64(win), 0, "e4m3").T @ xq + mxq(f64(vin), 0, "e4m3").T @ e_tok)
    g = np.tanh(mxq(f64(wca), 0, "e4m3").T @ xq + mxq(f64(vca), 0, "e4m3").T @ e_tok)
    new = old * f + a * g
    return b * np.tanh(new)

@@ -1,0 +1,189 @@
+from contextlib import ExitStack
+
+import concourse.mybir as mybir
+
+K, T, S, W, N = 512, 2048, 512, 1024, 256
+FLOPS = 8 * 2 * K * N * S
+
+F32 = mybir.dt.float32
+BF16 = mybir.dt.bfloat16
+I32 = mybir.dt.int32
+U32 = mybir.dt.uint32
+U16 = mybir.dt.uint16
+U8 = mybir.dt.uint8
+FP8X4 = mybir.dt.float8_e4m3fn_x4
+ACT = mybir.ActivationFunctionType
+ALU = mybir.AluOpType
+
+P = 128
+PACK = 4
+M_TILES = N // P
+HALF = S // 2
+
+
+def tile_picked_zlstm_std_p_kernel(
+    tc, x_words, x_scales, e_words, e_scales, win, vin, wfo, vfo, wex, vex, wca, vca, cell, offs, tok, out
+):
+    nc = tc.nc
+    with ExitStack() as ctx:
+        keep = ctx.enter_context(tc.tile_pool(name="keep", bufs=1))
+        psum = ctx.enter_context(tc.psum_pool(name="psum", bufs=1))
+
+        offs_t = keep.tile([P, S // 16], U16, name="offs_t")
+        tok_t = keep.tile([P, S // 16], U16, name="tok_t")
+        xw_t = keep.tile([P, T], I32, name="xw_t")
+        ew_t = keep.tile([P, W], I32, name="ew_t")
+        xs_t = keep.tile([P, T], U8, name="xs_t")
+        es_t = keep.tile([P, W], U8, name="es_t")
+        cell_t = [keep.tile([P, T], F32, name="cell%d" % m) for m in range(M_TILES)]
+        xg = keep.tile([P, S], U32, name="xg", align_bytes=64)
+        eg = keep.tile([P, S], U32, name="eg", align_bytes=64)
+        xsg = keep.tile([P, S], U8, name="xsg", align_bytes=64)
+        esg = keep.tile([P, S], U8, name="esg", align_bytes=64)
+
+        nc.vector.memset(es_t[:].bitcast(I32), 0)
+        nc.vector.memset(xs_t[:].bitcast(I32), 0)
+        warm = keep.tile([P, 1], F32, name="warm")
+        warm_out = keep.tile([P, 1], F32, name="warm_out")
+        nc.gpsimd.memset(warm[:], 0.0)
+        nc.scalar.activation(out=warm_out[:], in_=warm[:], func=ACT.Sigmoid)
+
+        weights = {"win": win, "vin": vin, "wfo": wfo, "vfo": vfo, "wex": wex, "vex": vex, "wca": wca, "vca": vca}
+        raw = {}
+
+        def load_weight(name):
+            raw[name] = keep.tile([P, PACK, N], F32, name="raw_" + name)
+            nc.sync.dma_start(out=raw[name][:], in_=weights[name].rearrange("(p j) n -> p j n", j=PACK))
+
+        def load_words(tile, words):
+            nc.sync.dma_start(out=tile[:], in_=words[0].rearrange("p n t -> p (n t)").bitcast(I32))
+
+        def load_scales(queue, tile, scales):
+            for r in range(4):
+                queue.dma_start(out=tile[r:P:32, :].bitcast(I32), in_=scales[0, r:16:4, :].bitcast(I32))
+
+        load_words(ew_t, e_words)
+        nc.sync.dma_start(tok_t[:], tok)
+        load_scales(nc.sync, es_t, e_scales)
+        load_words(xw_t, x_words)
+        nc.sync.dma_start(offs_t[:], offs)
+        load_scales(nc.sync, xs_t, x_scales)
+        for name in ("vca", "wca", "win", "vin", "wfo", "vfo"):
+            load_weight(name)
+        for m in range(M_TILES):
+            nc.sync.dma_start(out=cell_t[m][:], in_=cell[m * P : (m + 1) * P, :])
+        load_weight("wex")
+        load_weight("vex")
+
+        def interleave(name, c0, c1, on_scalar):
+            grouped = keep.tile([P, c1 - c0, PACK], BF16, name="grp_%s_%d" % (name, c0), align_bytes=64)
+            dst = grouped[:].rearrange("p (c i) t -> p c t i", i=4)
+            src = raw[name][:, :, c0:c1].rearrange("p t (c i) -> p c t i", i=4)
+            if on_scalar:
+                nc.scalar.copy(out=dst, in_=src)
+            else:
+                nc.vector.tensor_copy(out=dst, in_=src)
+            return grouped
+
+        def quantise(name, c0, grouped):
+            width = grouped.shape[1]
+            codes = keep.tile([P, width], U32, name="codes_%s_%d" % (name, c0), align_bytes=64)
+            scales = keep.tile([P, width], U8, name="scales_%s_%d" % (name, c0), align_bytes=64)
+            nc.vector.quantize_mx(
+                out=codes[:].bitcast(FP8X4), scales=scales[:], in_=grouped[:].rearrange("p c t -> p (c t)")
+            )
+            return codes, scales
+
+        x_side = (xg, xsg)
+        e_side = (eg, esg)
+
+        def gate_sum(acc, terms, rows, cols):
+            for i, (weight, side) in enumerate(terms):
+                nc.tensor.matmul_mx(
+                    out=acc, lhsT=weight[0][:, rows].bitcast(FP8X4), lhsT_scale=weight[1][:, rows],
+                    rhs=side[0][:, cols].bitcast(FP8X4), rhs_scale=side[1][:, cols], start=(i == 0), stop=(i == 1),
+                )
+
+        def gate(name, terms, func):
+            tiles = []
+            for m in range(M_TILES):
+                acc = psum.tile([P, S], F32, name="acc_%s%d" % (name, m))
+                gate_sum(acc[:], terms, slice(m * P, (m + 1) * P), slice(0, S))
+                val = keep.tile([P, S], F32, name="%s%d" % (name, m))
+                nc.scalar.activation(out=val[:], in_=acc[:], func=func)
+                tiles.append(val)
+            return tiles
+
+        nc.vector.tensor_copy(out=eg[:], in_=ew_t[:].bitcast(U32).indirect(tok_t[:]))
+        nc.vector.tensor_copy(out=esg[:], in_=es_t[:].indirect(tok_t[:]))
+        nc.vector.tensor_copy(out=xg[:], in_=xw_t[:].bitcast(U32).indirect(offs_t[:]))
+        nc.vector.tensor_copy(out=xsg[:], in_=xs_t[:].indirect(offs_t[:]))
+        grp_vca = interleave("vca", 0, N, True)
+        grp_wca = interleave("wca", 0, N, True)
+        q_vca = quantise("vca", 0, grp_vca)
+        q_wca = quantise("wca", 0, grp_wca)
+        g = gate("g", [(q_vca, e_side), (q_wca, x_side)], ACT.Tanh)
+        grp_win = interleave("win", 0, N, False)
+        q_win = quantise("win", 0, grp_win)
+        grp_vin = interleave("vin", 0, N, False)
+        q_vin = quantise("vin", 0, grp_vin)
+        grp_wfo = interleave("wfo", 0, N, True)
+        a = gate("a", [(q_win, x_side), (q_vin, e_side)], ACT.Sigmoid)
+        grp_vfo = interleave("vfo", 0, N, False)
+        q_wfo = quantise("wfo", 0, grp_wfo)
+        q_vfo = quantise("vfo", 0, grp_vfo)
+        f_terms = [(q_wfo, x_side), (q_vfo, e_side)]
+        ag_t = keep.tile([P, M_TILES * S], F32, name="grp_vfo_0", align_bytes=64)
+        ag = [ag_t[:, m * S : (m + 1) * S] for m in range(M_TILES)]
+        for m in range(M_TILES):
+            nc.vector.tensor_tensor(out=ag[m], in0=a[m][:], in1=g[m][:], op=ALU.mult)
+
+        halves = [slice(0, HALF), slice(HALF, S)]
+        rows = [slice(0, P), slice(P, N)]
+
+        kept0 = keep.tile([P, S], F32, name="kept0")
+        for h in range(2):
+            acc = psum.tile([P, HALF], F32, name="acc_f0%d" % h)
+            gate_sum(acc[:], f_terms, rows[0], halves[h])
+            f0 = keep.tile([P, HALF], F32, name="f0_%d" % h)
+            nc.scalar.activation(out=f0[:], in_=acc[:], func=ACT.Sigmoid)
+            nc.vector.tensor_tensor(
+                out=kept0[:, halves[h]], in0=cell_t[0][:].indirect(offs_t[:, 16 * h : 16 * (h + 1)]), in1=f0[:], op=ALU.mult
+            )
+        acc = psum.tile([P, S], F32, name="acc_f1")
+        gate_sum(acc[:], f_terms, rows[1], slice(0, S))
+        f1 = keep.tile([P, S], F32, name="f1")
+        nc.scalar.activation(out=f1[:], in_=acc[:], func=ACT.Sigmoid)
+        new0 = keep.tile([P, S], F32, name="new0")
+        nc.vector.tensor_tensor(out=new0[:], in0=kept0[:], in1=ag[0], op=ALU.add)
+        sq0 = keep.tile([P, S], F32, name="sq0")
+        nc.scalar.activation(out=sq0[:], in_=new0[:], func=ACT.Tanh)
+
+        kept1 = keep.tile([P, S], F32, name="kept1")
+        nc.vector.tensor_tensor(out=kept1[:], in0=cell_t[1][:].indirect(offs_t[:]), in1=f1[:], op=ALU.mult)
+
+        grp_wex = [interleave("wex", 0, P, True), interleave("wex", P, N, True)]
+        q_wex = [quantise("wex", 0, grp_wex[0])]
+        new1 = [grp_wex[0][:].rearrange("p c t -> p (c t)").bitcast(F32)]
+        nc.vector.tensor_tensor(out=new1[0], in0=kept1[:, halves[0]], in1=ag[1][:, halves[0]], op=ALU.add)
+        sq1 = [keep.tile([P, HALF], F32, name="sq1_%d" % h) for h in range(2)]
+        grp_vex0 = interleave("vex", 0, P, False)
+        q_wex.append(quantise("wex", P, grp_wex[1]))
+        q_vex = [quantise("vex", 0, grp_vex0)]
+        nc.scalar.activation(out=sq1[0][:], in_=new1[0], func=ACT.Tanh)
+        grp_vex1 = interleave("vex", P, N, True)
+        new1.append(grp_vex0[:].rearrange("p c t -> p (c t)").bitcast(F32))
+        nc.vector.tensor_tensor(out=new1[1], in0=kept1[:, halves[1]], in1=ag[1][:, halves[1]], op=ALU.add)
+        q_vex.append(quantise("vex", P, grp_vex1))
+        nc.scalar.activation(out=sq1[1][:], in_=new1[1], func=ACT.Tanh)
+        squashed = [[sq0[:, halves[0]], sq0[:, halves[1]]], [sq1[0][:], sq1[1][:]]]
+        banks = ["acc_g0", "acc_g1", "acc_a0", "acc_a1"]
+        for m in range(M_TILES):
+            for h in range(2):
+                acc = psum.tile([P, HALF], F32, name=banks[2 * m + h])
+                gate_sum(acc[:], [(q_wex[m], x_side), (q_vex[m], e_side)], rows[0], halves[h])
+                b = keep.tile([P, HALF], F32, name="b%d_%d" % (m, h))
+                nc.scalar.activation(out=b[:], in_=acc[:], func=ACT.Sigmoid)
+                res = keep.tile([P, HALF], F32, name="res%d_%d" % (m, h))
+                nc.vector.tensor_tensor(out=res[:], in0=b[:], in1=squashed[m][h], op=ALU.mult)
+                nc.sync.dma_start(out=out[rows[m], halves[h]], in_=res[:])

@@ -19,6 +19,7 @@ P = 128
 PACK = 4
 M_TILES = N // P
 HALF = S // 2
+E_ROW = 4
 
 
 def tile_picked_zlstm_std_p_kernel(
@@ -58,16 +59,16 @@ def tile_picked_zlstm_std_p_kernel(
         def load_words(tile, words):
             nc.sync.dma_start(out=tile[:], in_=words[0].rearrange("p n t -> p (n t)").bitcast(I32))
 
-        def load_scales(queue, tile, scales):
+        def load_scales(tile, scales, first):
             for r in range(4):
-                queue.dma_start(out=tile[r:P:32, :].bitcast(I32), in_=scales[0, r:16:4, :].bitcast(I32))
+                nc.sync.dma_start(out=tile[first + r : P : 32, :].bitcast(I32), in_=scales[0, r:16:4, :].bitcast(I32))
 
         load_words(ew_t, e_words)
         nc.sync.dma_start(tok_t[:], tok)
-        load_scales(nc.sync, es_t, e_scales)
+        load_scales(es_t, e_scales, E_ROW)
         load_words(xw_t, x_words)
         nc.sync.dma_start(offs_t[:], offs)
-        load_scales(nc.sync, xs_t, x_scales)
+        load_scales(xs_t, x_scales, 0)
         for name in ("vca", "wca", "win", "vin", "wfo", "vfo"):
             load_weight(name)
         for m in range(M_TILES):
@@ -94,8 +95,8 @@ def tile_picked_zlstm_std_p_kernel(
             )
             return codes, scales
 
-        x_side = (xg, xsg)
-        e_side = (eg, esg)
+        x_side = (xg[:], xsg[:])
+        e_side = (eg[:], esg[E_ROW:P, :])
 
         def gate_sum(acc, terms, rows, cols):
             for i, (weight, side) in enumerate(terms):
@@ -162,28 +163,37 @@ def tile_picked_zlstm_std_p_kernel(
         kept1 = keep.tile([P, S], F32, name="kept1")
         nc.vector.tensor_tensor(out=kept1[:], in0=cell_t[1][:].indirect(offs_t[:]), in1=f1[:], op=ALU.mult)
 
+        def spent(name, c0):
+            return raw[name][:, 0:2, c0 : c0 + P]
+
+        def two_runs(ap):
+            return ap.rearrange("p (u c) -> p u c", u=2)
+
         grp_wex = [interleave("wex", 0, P, True), interleave("wex", P, N, True)]
         q_wex = [quantise("wex", 0, grp_wex[0])]
-        new1 = [grp_wex[0][:].rearrange("p c t -> p (c t)").bitcast(F32)]
-        nc.vector.tensor_tensor(out=new1[0], in0=kept1[:, halves[0]], in1=ag[1][:, halves[0]], op=ALU.add)
-        sq1 = [keep.tile([P, HALF], F32, name="sq1_%d" % h) for h in range(2)]
+        new1 = [spent("wex", 0), spent("vex", 0)]
+        nc.vector.tensor_tensor(out=new1[0], in0=two_runs(kept1[:, halves[0]]), in1=two_runs(ag[1][:, halves[0]]), op=ALU.add)
         grp_vex0 = interleave("vex", 0, P, False)
         q_wex.append(quantise("wex", P, grp_wex[1]))
         q_vex = [quantise("vex", 0, grp_vex0)]
-        nc.scalar.activation(out=sq1[0][:], in_=new1[0], func=ACT.Tanh)
         grp_vex1 = interleave("vex", P, N, True)
-        new1.append(grp_vex0[:].rearrange("p c t -> p (c t)").bitcast(F32))
-        nc.vector.tensor_tensor(out=new1[1], in0=kept1[:, halves[1]], in1=ag[1][:, halves[1]], op=ALU.add)
+        sq1 = [spent("vex", P), spent("wex", P)]
+        nc.scalar.activation(out=sq1[0], in_=new1[0], func=ACT.Tanh)
+        nc.vector.tensor_tensor(out=new1[1], in0=two_runs(kept1[:, halves[1]]), in1=two_runs(ag[1][:, halves[1]]), op=ALU.add)
         q_vex.append(quantise("vex", P, grp_vex1))
-        nc.scalar.activation(out=sq1[1][:], in_=new1[1], func=ACT.Tanh)
-        squashed = [[sq0[:, halves[0]], sq0[:, halves[1]]], [sq1[0][:], sq1[1][:]]]
-        banks = ["acc_g0", "acc_g1", "acc_a0", "acc_a1"]
-        for m in range(M_TILES):
-            for h in range(2):
-                acc = psum.tile([P, HALF], F32, name=banks[2 * m + h])
-                gate_sum(acc[:], [(q_wex[m], x_side), (q_vex[m], e_side)], rows[0], halves[h])
-                b = keep.tile([P, HALF], F32, name="b%d_%d" % (m, h))
-                nc.scalar.activation(out=b[:], in_=acc[:], func=ACT.Sigmoid)
-                res = keep.tile([P, HALF], F32, name="res%d_%d" % (m, h))
-                nc.vector.tensor_tensor(out=res[:], in0=b[:], in1=squashed[m][h], op=ALU.mult)
-                nc.sync.dma_start(out=out[rows[m], halves[h]], in_=res[:])
+        nc.scalar.activation(out=sq1[1], in_=new1[1], func=ACT.Tanh)
+        pieces = [
+            (0, 0, HALF, two_runs(sq0[:, halves[0]]), "acc_g0"),
+            (0, HALF, S, two_runs(sq0[:, halves[1]]), "acc_g1"),
+            (1, 0, HALF, sq1[0], "acc_a0"),
+            (1, HALF, HALF + P, two_runs(sq1[1][:, 0, :]), "acc_a1"),
+            (1, HALF + P, S, two_runs(sq1[1][:, 1, :]), "acc_f00"),
+        ]
+        for m, c0, c1, squashed, bank in pieces:
+            acc = psum.tile([P, c1 - c0], F32, name=bank)
+            gate_sum(acc[:], [(q_wex[m], x_side), (q_vex[m], e_side)], rows[0], slice(c0, c1))
+            b = keep.tile([P, c1 - c0], F32, name="b%d_%d" % (m, c0))
+            nc.scalar.activation(out=b[:], in_=acc[:], func=ACT.Sigmoid)
+            res = keep.tile([P, c1 - c0], F32, name="res%d_%d" % (m, c0))
+            nc.vector.tensor_tensor(out=two_runs(res[:]), in0=two_runs(b[:]), in1=squashed, op=ALU.mult)
+            nc.sync.dma_start(out=out[rows[m], c0:c1], in_=res[:])

@@ -124,23 +124,25 @@ def tile_picked_zlstm_std_p_kernel(
         q_vca = quantise("vca", 0, grp_vca)
         q_wca = quantise("wca", 0, grp_wca)
         g = gate("g", [(q_vca, e_side), (q_wca, x_side)], ACT.Tanh)
-        grp_win = interleave("win", 0, N, False)
-        q_win = quantise("win", 0, grp_win)
+        grp_win = interleave("win", 0, N, True)
         grp_vin = interleave("vin", 0, N, False)
+        q_win = quantise("win", 0, grp_win)
         q_vin = quantise("vin", 0, grp_vin)
         grp_wfo = interleave("wfo", 0, N, True)
         a = gate("a", [(q_win, x_side), (q_vin, e_side)], ACT.Sigmoid)
         grp_vfo = interleave("vfo", 0, N, False)
         q_wfo = quantise("wfo", 0, grp_wfo)
         q_vfo = quantise("vfo", 0, grp_vfo)
-        f_terms = [(q_wfo, x_side), (q_vfo, e_side)]
-        ag_t = keep.tile([P, M_TILES * S], F32, name="grp_vfo_0", align_bytes=64)
-        ag = [ag_t[:, m * S : (m + 1) * S] for m in range(M_TILES)]
-        for m in range(M_TILES):
-            nc.vector.tensor_tensor(out=ag[m], in0=a[m][:], in1=g[m][:], op=ALU.mult)
 
         halves = [slice(0, HALF), slice(HALF, S)]
         rows = [slice(0, P), slice(P, N)]
+        f_terms = [(q_wfo, x_side), (q_vfo, e_side)]
+
+        ag = []
+        for m in range(M_TILES):
+            prod = keep.tile([P, S], F32, name="ag%d" % m)
+            nc.vector.tensor_tensor(out=prod[:], in0=a[m][:], in1=g[m][:], op=ALU.mult)
+            ag.append(prod)
 
         kept0 = keep.tile([P, S], F32, name="kept0")
         for h in range(2):
@@ -156,7 +158,8 @@ def tile_picked_zlstm_std_p_kernel(
         f1 = keep.tile([P, S], F32, name="f1")
         nc.scalar.activation(out=f1[:], in_=acc[:], func=ACT.Sigmoid)
         new0 = keep.tile([P, S], F32, name="new0")
-        nc.vector.tensor_tensor(out=new0[:], in0=kept0[:], in1=ag[0], op=ALU.add)
+        for h in range(2):
+            nc.vector.tensor_tensor(out=new0[:, halves[h]], in0=kept0[:, halves[h]], in1=ag[0][:, halves[h]], op=ALU.add)
         sq0 = keep.tile([P, S], F32, name="sq0")
         nc.scalar.activation(out=sq0[:], in_=new0[:], func=ACT.Tanh)
 

@@ -180,19 +180,12 @@ def tile_picked_zlstm_std_p_kernel(
         q_wex.append(quantise("wex", P, grp_wex[1]))
         q_vex = [quantise("vex", 0, grp_vex0)]
         grp_vex1 = interleave("vex", P, N, True)
-        sq1 = [spent("vex", P), spent("wex", P)]
-        nc.scalar.activation(out=sq1[0], in_=new1[0], func=ACT.Tanh)
+        sq1_first = spent("vex", P)
+        nc.scalar.activation(out=sq1_first, in_=new1[0], func=ACT.Tanh)
         nc.vector.tensor_tensor(out=new1[1], in0=two_runs(kept1[:, halves[1]]), in1=two_runs(ag[1][:, halves[1]]), op=ALU.add)
         q_vex.append(quantise("vex", P, grp_vex1))
-        nc.scalar.activation(out=sq1[1], in_=new1[1], func=ACT.Tanh)
-        pieces = [
-            (0, 0, HALF, two_runs(sq0[:, halves[0]]), "acc_g0"),
-            (0, HALF, S, two_runs(sq0[:, halves[1]]), "acc_g1"),
-            (1, 0, HALF, sq1[0], "acc_a0"),
-            (1, HALF, HALF + P, two_runs(sq1[1][:, 0, :]), "acc_a1"),
-            (1, HALF + P, S, two_runs(sq1[1][:, 1, :]), "acc_f00"),
-        ]
-        for m, c0, c1, squashed, bank in pieces:
+
+        def finish(m, c0, c1, squashed, bank):
             acc = psum.tile([P, c1 - c0], F32, name=bank)
             gate_sum(acc[:], [(q_wex[m], x_side), (q_vex[m], e_side)], rows[0], slice(c0, c1))
             b = keep.tile([P, c1 - c0], F32, name="b%d_%d" % (m, c0))
@@ -200,3 +193,12 @@ def tile_picked_zlstm_std_p_kernel(
             res = keep.tile([P, c1 - c0], F32, name="res%d_%d" % (m, c0))
             nc.vector.tensor_tensor(out=two_runs(res[:]), in0=two_runs(b[:]), in1=squashed, op=ALU.mult)
             nc.sync.dma_start(out=out[rows[m], c0:c1], in_=res[:])
+
+        finish(0, 0, P, two_runs(sq0[:, 0:P]), "acc_g0")
+        sq1_second = keep.tile([P, HALF], F32, name="b0_0")
+        nc.scalar.activation(out=two_runs(sq1_second[:]), in_=new1[1], func=ACT.Tanh)
+        finish(0, P, HALF, two_runs(sq0[:, P:HALF]), "acc_f01")
+        finish(0, HALF, S, two_runs(sq0[:, halves[1]]), "acc_g1")
+        finish(1, 0, HALF, sq1_first, "acc_a0")
+        finish(1, HALF, HALF + P, two_runs(sq1_second[:, 0:P]), "acc_a1")
+        finish(1, HALF + P, S, two_runs(sq1_second[:, P:HALF]), "acc_f00")

@@ -18,8 +18,8 @@ ALU = mybir.AluOpType
 P = 128
 PACK = 4
 M_TILES = N // P
-HALF = S // 2
 E_ROW = 4
+LAST_PIECES = (256, 128, 128)
 
 
 def tile_picked_zlstm_std_p_kernel(
@@ -66,30 +66,28 @@ def tile_picked_zlstm_std_p_kernel(
         load_words(ew_t, e_words)
         nc.sync.dma_start(tok_t[:], tok)
         load_scales(es_t, e_scales, E_ROW)
+        load_weight("vca")
         load_words(xw_t, x_words)
         nc.sync.dma_start(offs_t[:], offs)
         load_scales(xs_t, x_scales, 0)
-        for name in ("vca", "wca", "win", "vin", "wfo", "vfo"):
+        for name in ("wca", "win", "vin", "wfo", "vfo", "wex", "vex"):
             load_weight(name)
         for m in range(M_TILES):
             nc.sync.dma_start(out=cell_t[m][:], in_=cell[m * P : (m + 1) * P, :])
-        load_weight("wex")
-        load_weight("vex")
 
-        def interleave(name, c0, c1, on_scalar):
-            grouped = keep.tile([P, c1 - c0, PACK], BF16, name="grp_%s_%d" % (name, c0), align_bytes=64)
+        def interleave(name, on_scalar):
+            grouped = keep.tile([P, N, PACK], BF16, name="grp_" + name, align_bytes=64)
             dst = grouped[:].rearrange("p (c i) t -> p c t i", i=4)
-            src = raw[name][:, :, c0:c1].rearrange("p t (c i) -> p c t i", i=4)
+            src = raw[name][:].rearrange("p t (c i) -> p c t i", i=4)
             if on_scalar:
                 nc.scalar.copy(out=dst, in_=src)
             else:
                 nc.vector.tensor_copy(out=dst, in_=src)
             return grouped
 
-        def quantise(name, c0, grouped):
-            width = grouped.shape[1]
-            codes = keep.tile([P, width], U32, name="codes_%s_%d" % (name, c0), align_bytes=64)
-            scales = keep.tile([P, width], U8, name="scales_%s_%d" % (name, c0), align_bytes=64)
+        def quantise(name, grouped):
+            codes = keep.tile([P, N], U32, name="codes_" + name, align_bytes=64)
+            scales = keep.tile([P, N], U8, name="scales_" + name, align_bytes=64)
             nc.vector.quantize_mx(
                 out=codes[:].bitcast(FP8X4), scales=scales[:], in_=grouped[:].rearrange("p c t -> p (c t)")
             )
@@ -98,18 +96,21 @@ def tile_picked_zlstm_std_p_kernel(
         x_side = (xg[:], xsg[:])
         e_side = (eg[:], esg[E_ROW:P, :])
 
-        def gate_sum(acc, terms, rows, cols):
-            for i, (weight, side) in enumerate(terms):
-                nc.tensor.matmul_mx(
-                    out=acc, lhsT=weight[0][:, rows].bitcast(FP8X4), lhsT_scale=weight[1][:, rows],
-                    rhs=side[0][:, cols].bitcast(FP8X4), rhs_scale=side[1][:, cols], start=(i == 0), stop=(i == 1),
-                )
-
-        def gate(name, terms, func):
+        def gate(name, first, second, func, both_on_scalar=False):
+            grouped = [interleave(first, True), interleave(second, both_on_scalar)]
+            terms = [
+                (quantise(w_name, grp), x_side if w_name[0] == "w" else e_side)
+                for w_name, grp in zip((first, second), grouped)
+            ]
             tiles = []
             for m in range(M_TILES):
+                rows = slice(m * P, (m + 1) * P)
                 acc = psum.tile([P, S], F32, name="acc_%s%d" % (name, m))
-                gate_sum(acc[:], terms, slice(m * P, (m + 1) * P), slice(0, S))
+                for i, (weight, side) in enumerate(terms):
+                    nc.tensor.matmul_mx(
+                        out=acc[:], lhsT=weight[0][:, rows].bitcast(FP8X4), lhsT_scale=weight[1][:, rows],
+                        rhs=side[0].bitcast(FP8X4), rhs_scale=side[1], start=(i == 0), stop=(i == 1),
+                    )
                 val = keep.tile([P, S], F32, name="%s%d" % (name, m))
                 nc.scalar.activation(out=val[:], in_=acc[:], func=func)
                 tiles.append(val)
@@ -119,86 +120,45 @@ def tile_picked_zlstm_std_p_kernel(
         nc.vector.tensor_copy(out=esg[:], in_=es_t[:].indirect(tok_t[:]))
         nc.vector.tensor_copy(out=xg[:], in_=xw_t[:].bitcast(U32).indirect(offs_t[:]))
         nc.vector.tensor_copy(out=xsg[:], in_=xs_t[:].indirect(offs_t[:]))
-        grp_vca = interleave("vca", 0, N, True)
-        grp_wca = interleave("wca", 0, N, True)
-        q_vca = quantise("vca", 0, grp_vca)
-        q_wca = quantise("wca", 0, grp_wca)
-        g = gate("g", [(q_vca, e_side), (q_wca, x_side)], ACT.Tanh)
-        grp_win = interleave("win", 0, N, True)
-        grp_vin = interleave("vin", 0, N, False)
-        q_win = quantise("win", 0, grp_win)
-        q_vin = quantise("vin", 0, grp_vin)
-        grp_wfo = interleave("wfo", 0, N, True)
-        a = gate("a", [(q_win, x_side), (q_vin, e_side)], ACT.Sigmoid)
-        grp_vfo = interleave("vfo", 0, N, False)
-        q_wfo = quantise("wfo", 0, grp_wfo)
-        q_vfo = quantise("vfo", 0, grp_vfo)
-
-        halves = [slice(0, HALF), slice(HALF, S)]
-        rows = [slice(0, P), slice(P, N)]
-        f_terms = [(q_wfo, x_side), (q_vfo, e_side)]
-
+        g = gate("g", "vca", "wca", ACT.Tanh, True)
+        a = gate("a", "win", "vin", ACT.Sigmoid)
+        f = gate("f", "wfo", "vfo", ACT.Sigmoid)
+        b = gate("b", "wex", "vex", ACT.Sigmoid)
         ag = []
         for m in range(M_TILES):
-            prod = keep.tile([P, S], F32, name="ag%d" % m)
-            nc.vector.tensor_tensor(out=prod[:], in0=a[m][:], in1=g[m][:], op=ALU.mult)
+            prod = raw[("vfo", "vex")[m]][:].rearrange("p j n -> p (j n)")[:, 0:S]
+            nc.vector.tensor_tensor(out=prod, in0=a[m][:], in1=g[m][:], op=ALU.mult)
             ag.append(prod)
 
-        kept0 = keep.tile([P, S], F32, name="kept0")
-        for h in range(2):
-            acc = psum.tile([P, HALF], F32, name="acc_f0%d" % h)
-            gate_sum(acc[:], f_terms, rows[0], halves[h])
-            f0 = keep.tile([P, HALF], F32, name="f0_%d" % h)
-            nc.scalar.activation(out=f0[:], in_=acc[:], func=ACT.Sigmoid)
-            nc.vector.tensor_tensor(
-                out=kept0[:, halves[h]], in0=cell_t[0][:].indirect(offs_t[:, 16 * h : 16 * (h + 1)]), in1=f0[:], op=ALU.mult
-            )
-        acc = psum.tile([P, S], F32, name="acc_f1")
-        gate_sum(acc[:], f_terms, rows[1], slice(0, S))
-        f1 = keep.tile([P, S], F32, name="f1")
-        nc.scalar.activation(out=f1[:], in_=acc[:], func=ACT.Sigmoid)
-        new0 = keep.tile([P, S], F32, name="new0")
-        for h in range(2):
-            nc.vector.tensor_tensor(out=new0[:, halves[h]], in0=kept0[:, halves[h]], in1=ag[0][:, halves[h]], op=ALU.add)
-        sq0 = keep.tile([P, S], F32, name="sq0")
-        nc.scalar.activation(out=sq0[:], in_=new0[:], func=ACT.Tanh)
+        def finish(m, widths):
+            starts = [sum(widths[:i]) for i in range(len(widths))]
+            cols = [slice(c0, c0 + w) for c0, w in zip(starts, widths)]
+            kept, new, squashed = {}, {}, {}
 
-        kept1 = keep.tile([P, S], F32, name="kept1")
-        nc.vector.tensor_tensor(out=kept1[:], in0=cell_t[1][:].indirect(offs_t[:]), in1=f1[:], op=ALU.mult)
+            def keep_old(i):
+                kept[i] = keep.tile([P, widths[i]], F32, name="kept%d_%d" % (m, i))
+                window = cell_t[m][:].indirect(offs_t[:, cols[i].start // 16 : cols[i].stop // 16])
+                nc.vector.tensor_tensor(out=kept[i][:], in0=window, in1=f[m][:, cols[i]], op=ALU.mult)
 
-        def spent(name, c0):
-            return raw[name][:, 0:2, c0 : c0 + P]
+            def renew(i):
+                new[i] = keep.tile([P, widths[i]], F32, name="new%d_%d" % (m, i))
+                nc.vector.tensor_tensor(out=new[i][:], in0=kept[i][:], in1=ag[m][:, cols[i]], op=ALU.add)
+                squashed[i] = keep.tile([P, widths[i]], F32, name="sq%d_%d" % (m, i))
+                nc.scalar.activation(out=squashed[i][:], in_=new[i][:], func=ACT.Tanh)
 
-        def two_runs(ap):
-            return ap.rearrange("p (u c) -> p u c", u=2)
+            def emit(i):
+                res = keep.tile([P, widths[i]], F32, name="res%d_%d" % (m, i))
+                nc.vector.tensor_tensor(out=res[:], in0=b[m][:, cols[i]], in1=squashed[i][:], op=ALU.mult)
+                nc.sync.dma_start(out=out[m * P : (m + 1) * P, cols[i]], in_=res[:])
 
-        grp_wex = [interleave("wex", 0, P, True), interleave("wex", P, N, True)]
-        q_wex = [quantise("wex", 0, grp_wex[0])]
-        new1 = [spent("wex", 0), spent("vex", 0)]
-        nc.vector.tensor_tensor(out=new1[0], in0=two_runs(kept1[:, halves[0]]), in1=two_runs(ag[1][:, halves[0]]), op=ALU.add)
-        grp_vex0 = interleave("vex", 0, P, False)
-        q_wex.append(quantise("wex", P, grp_wex[1]))
-        q_vex = [quantise("vex", 0, grp_vex0)]
-        grp_vex1 = interleave("vex", P, N, True)
-        sq1_first = spent("vex", P)
-        nc.scalar.activation(out=sq1_first, in_=new1[0], func=ACT.Tanh)
-        nc.vector.tensor_tensor(out=new1[1], in0=two_runs(kept1[:, halves[1]]), in1=two_runs(ag[1][:, halves[1]]), op=ALU.add)
-        q_vex.append(quantise("vex", P, grp_vex1))
+            n = len(widths)
+            for step in range(n + 2):
+                if step < n:
+                    keep_old(step)
+                if 1 <= step <= n:
+                    renew(step - 1)
+                if step >= 2:
+                    emit(step - 2)
 
-        def finish(m, c0, c1, squashed, bank):
-            acc = psum.tile([P, c1 - c0], F32, name=bank)
-            gate_sum(acc[:], [(q_wex[m], x_side), (q_vex[m], e_side)], rows[0], slice(c0, c1))
-            b = keep.tile([P, c1 - c0], F32, name="b%d_%d" % (m, c0))
-            nc.scalar.activation(out=b[:], in_=acc[:], func=ACT.Sigmoid)
-            res = keep.tile([P, c1 - c0], F32, name="res%d_%d" % (m, c0))
-            nc.vector.tensor_tensor(out=two_runs(res[:]), in0=two_runs(b[:]), in1=squashed, op=ALU.mult)
-            nc.sync.dma_start(out=out[rows[m], c0:c1], in_=res[:])
-
-        finish(0, 0, P, two_runs(sq0[:, 0:P]), "acc_g0")
-        sq1_second = keep.tile([P, HALF], F32, name="b0_0")
-        nc.scalar.activation(out=two_runs(sq1_second[:]), in_=new1[1], func=ACT.Tanh)
-        finish(0, P, HALF, two_runs(sq0[:, P:HALF]), "acc_f01")
-        finish(0, HALF, S, two_runs(sq0[:, halves[1]]), "acc_g1")
-        finish(1, 0, HALF, sq1_first, "acc_a0")
-        finish(1, HALF, HALF + P, two_runs(sq1_second[:, 0:P]), "acc_a1")
-        finish(1, HALF + P, S, two_runs(sq1_second[:, P:HALF]), "acc_f00")
+        finish(0, (256, 256))
+        finish(1, LAST_PIECES)

@@ -19,7 +19,8 @@ P = 128
 PACK = 4
 M_TILES = N // P
 E_ROW = 4
-LAST_PIECES = (256, 128, 128)
+PIECE = 128
+STORE_AT = ((512,), (256, 384, 512))
 
 
 def tile_picked_zlstm_std_p_kernel(
@@ -130,35 +131,26 @@ def tile_picked_zlstm_std_p_kernel(
             nc.vector.tensor_tensor(out=prod, in0=a[m][:], in1=g[m][:], op=ALU.mult)
             ag.append(prod)
 
-        def finish(m, widths):
-            starts = [sum(widths[:i]) for i in range(len(widths))]
-            cols = [slice(c0, c0 + w) for c0, w in zip(starts, widths)]
-            kept, new, squashed = {}, {}, {}
+        def finish(m):
+            kept = keep.tile([P, S], F32, name="kept%d" % m)
+            new = keep.tile([P, S], F32, name="new%d" % m)
+            squashed = keep.tile([P, S], F32, name="sq%d" % m)
+            res = keep.tile([P, S], F32, name="res%d" % m)
+            for c0 in range(0, S, S // 2):
+                cols = slice(c0, c0 + S // 2)
+                window = cell_t[m][:].indirect(offs_t[:, cols.start // 16 : cols.stop // 16])
+                nc.vector.tensor_tensor(out=kept[:, cols], in0=window, in1=f[m][:, cols], op=ALU.mult)
+            for c0 in range(0, S, PIECE):
+                cols = slice(c0, c0 + PIECE)
+                nc.vector.tensor_tensor(out=new[:, cols], in0=kept[:, cols], in1=ag[m][:, cols], op=ALU.add)
+                nc.scalar.activation(out=squashed[:, cols], in_=new[:, cols], func=ACT.Tanh)
+            stored = 0
+            for c0 in range(0, S, PIECE):
+                cols = slice(c0, c0 + PIECE)
+                nc.vector.tensor_tensor(out=res[:, cols], in0=b[m][:, cols], in1=squashed[:, cols], op=ALU.mult)
+                if cols.stop in STORE_AT[m]:
+                    nc.sync.dma_start(out=out[m * P : (m + 1) * P, stored : cols.stop], in_=res[:, stored : cols.stop])
+                    stored = cols.stop
 
-            def keep_old(i):
-                kept[i] = keep.tile([P, widths[i]], F32, name="kept%d_%d" % (m, i))
-                window = cell_t[m][:].indirect(offs_t[:, cols[i].start // 16 : cols[i].stop // 16])
-                nc.vector.tensor_tensor(out=kept[i][:], in0=window, in1=f[m][:, cols[i]], op=ALU.mult)
-
-            def renew(i):
-                new[i] = keep.tile([P, widths[i]], F32, name="new%d_%d" % (m, i))
-                nc.vector.tensor_tensor(out=new[i][:], in0=kept[i][:], in1=ag[m][:, cols[i]], op=ALU.add)
-                squashed[i] = keep.tile([P, widths[i]], F32, name="sq%d_%d" % (m, i))
-                nc.scalar.activation(out=squashed[i][:], in_=new[i][:], func=ACT.Tanh)
-
-            def emit(i):
-                res = keep.tile([P, widths[i]], F32, name="res%d_%d" % (m, i))
-                nc.vector.tensor_tensor(out=res[:], in0=b[m][:, cols[i]], in1=squashed[i][:], op=ALU.mult)
-                nc.sync.dma_start(out=out[m * P : (m + 1) * P, cols[i]], in_=res[:])
-
-            n = len(widths)
-            for step in range(n + 2):
-                if step < n:
-                    keep_old(step)
-                if 1 <= step <= n:
-                    renew(step - 1)
-                if step >= 2:
-                    emit(step - 2)
-
-        finish(0, (256, 256))
-        finish(1, LAST_PIECES)
+        for m in range(M_TILES):
+            finish(m)

@@ -18,9 +18,8 @@ ALU = mybir.AluOpType
 P = 128
 PACK = 4
 M_TILES = N // P
-E_ROW = 4
-PIECE = 128
-STORE_AT = ((512,), (256, 384, 512))
+EDGES = (0, 128, 256, 384, 448, 512)
+STORE_AT = ((512,), (256, 512))
 
 
 def tile_picked_zlstm_std_p_kernel(
@@ -29,52 +28,48 @@ def tile_picked_zlstm_std_p_kernel(
     nc = tc.nc
     with ExitStack() as ctx:
         keep = ctx.enter_context(tc.tile_pool(name="keep", bufs=1))
+        reuse = ctx.enter_context(tc.tile_pool(name="reuse", bufs=1))
         psum = ctx.enter_context(tc.psum_pool(name="psum", bufs=1))
 
         offs_t = keep.tile([P, S // 16], U16, name="offs_t")
         tok_t = keep.tile([P, S // 16], U16, name="tok_t")
-        xw_t = keep.tile([P, T], I32, name="xw_t")
-        ew_t = keep.tile([P, W], I32, name="ew_t")
-        xs_t = keep.tile([P, T], U8, name="xs_t")
+        xw_t = reuse.tile([P, T], I32, name="xw_t", align_bytes=64, offset=20480)
+        ew_t = reuse.tile([P, W], I32, name="ew_t", align_bytes=64, offset=10240)
+        xs_t = reuse.tile([P, T], U8, name="xs_t", align_bytes=64, offset=2048)
         es_t = keep.tile([P, W], U8, name="es_t")
-        cell_t = [keep.tile([P, T], F32, name="cell%d" % m) for m in range(M_TILES)]
         xg = keep.tile([P, S], U32, name="xg", align_bytes=64)
-        eg = keep.tile([P, S], U32, name="eg", align_bytes=64)
-        xsg = keep.tile([P, S], U8, name="xsg", align_bytes=64)
-        esg = keep.tile([P, S], U8, name="esg", align_bytes=64)
+        eg = reuse.tile([P, S], U32, name="eg", align_bytes=64, offset=64)
+        picked = keep.tile([P, 2 * S], U8, name="picked", align_bytes=64)
+        planes = keep.tile([P, 2 * S], U8, name="planes", align_bytes=64)
 
-        nc.vector.memset(es_t[:].bitcast(I32), 0)
-        nc.vector.memset(xs_t[:].bitcast(I32), 0)
         warm = keep.tile([P, 1], F32, name="warm")
         warm_out = keep.tile([P, 1], F32, name="warm_out")
         nc.gpsimd.memset(warm[:], 0.0)
         nc.scalar.activation(out=warm_out[:], in_=warm[:], func=ACT.Sigmoid)
+        nc.vector.memset(es_t[:].bitcast(I32), 0)
+        nc.vector.memset(xs_t[:].bitcast(I32), 0)
+        nc.vector.memset(planes[:].bitcast(I32), 0)
 
         weights = {"win": win, "vin": vin, "wfo": wfo, "vfo": vfo, "wex": wex, "vex": vex, "wca": wca, "vca": vca}
         raw = {}
 
-        def load_weight(name):
-            raw[name] = keep.tile([P, PACK, N], F32, name="raw_" + name)
+        def load_weight(name, slot=None, offset=None):
+            if offset is None:
+                raw[name] = keep.tile([P, PACK, N], F32, name="raw_" + name, tag=slot or "raw_" + name, align_bytes=64)
+            else:
+                raw[name] = reuse.tile([P, PACK, N], F32, name="raw_" + name, align_bytes=64, offset=offset)
             nc.sync.dma_start(out=raw[name][:], in_=weights[name].rearrange("(p j) n -> p j n", j=PACK))
 
         def load_words(tile, words):
             nc.sync.dma_start(out=tile[:], in_=words[0].rearrange("p n t -> p (n t)").bitcast(I32))
 
-        def load_scales(tile, scales, first):
-            for r in range(4):
-                nc.sync.dma_start(out=tile[first + r : P : 32, :].bitcast(I32), in_=scales[0, r:16:4, :].bitcast(I32))
+        def load_scales(tile, scales):
+            nc.sync.dma_start(out=tile[32:96:4, :].bitcast(I32), in_=scales[0].bitcast(I32))
 
-        load_words(ew_t, e_words)
-        nc.sync.dma_start(tok_t[:], tok)
-        load_scales(es_t, e_scales, E_ROW)
-        load_weight("vca")
-        load_words(xw_t, x_words)
-        nc.sync.dma_start(offs_t[:], offs)
-        load_scales(xs_t, x_scales, 0)
-        for name in ("wca", "win", "vin", "wfo", "vfo", "wex", "vex"):
-            load_weight(name)
-        for m in range(M_TILES):
-            nc.sync.dma_start(out=cell_t[m][:], in_=cell[m * P : (m + 1) * P, :])
+        def load_cell(m, slot):
+            tile = keep.tile([P, T], F32, name="cell%d" % m, tag=slot, align_bytes=64)
+            nc.sync.dma_start(out=tile[:], in_=cell[m * P : (m + 1) * P, :])
+            return tile
 
         def interleave(name, on_scalar):
             grouped = keep.tile([P, N, PACK], BF16, name="grp_" + name, align_bytes=64)
@@ -88,21 +83,19 @@ def tile_picked_zlstm_std_p_kernel(
 
         def quantise(name, grouped):
             codes = keep.tile([P, N], U32, name="codes_" + name, align_bytes=64)
-            scales = keep.tile([P, N], U8, name="scales_" + name, align_bytes=64)
+            if name in ("vca", "wca"):
+                scales = reuse.tile([P, N], U8, name="scales_" + name, align_bytes=64, offset=2560 + 256 * (name == "wca"))
+            else:
+                scales = keep.tile([P, N], U8, name="scales_" + name, align_bytes=64)
             nc.vector.quantize_mx(
                 out=codes[:].bitcast(FP8X4), scales=scales[:], in_=grouped[:].rearrange("p c t -> p (c t)")
             )
             return codes, scales
 
-        x_side = (xg[:], xsg[:])
-        e_side = (eg[:], esg[E_ROW:P, :])
+        x_side = (xg[:], planes[:, 0:S])
+        e_side = (eg[:], planes[:, S : 2 * S])
 
-        def gate(name, first, second, func, both_on_scalar=False):
-            grouped = [interleave(first, True), interleave(second, both_on_scalar)]
-            terms = [
-                (quantise(w_name, grp), x_side if w_name[0] == "w" else e_side)
-                for w_name, grp in zip((first, second), grouped)
-            ]
+        def gate(name, terms, func):
             tiles = []
             for m in range(M_TILES):
                 rows = slice(m * P, (m + 1) * P)
@@ -117,18 +110,41 @@ def tile_picked_zlstm_std_p_kernel(
                 tiles.append(val)
             return tiles
 
+        def prepare(name, on_scalar):
+            return quantise(name, interleave(name, on_scalar)), x_side if name[0] == "w" else e_side
+
+        load_weight("vca")
+        nc.sync.dma_start(tok_t[:], tok)
+        nc.sync.dma_start(offs_t[:], offs)
+        load_scales(es_t, e_scales)
+        load_words(ew_t, e_words)
+        load_scales(xs_t, x_scales)
+        load_words(xw_t, x_words)
+        load_weight("wca")
+        load_weight("win")
+
+        nc.vector.tensor_copy(out=picked[:, S : 2 * S], in_=es_t[:].indirect(tok_t[:]))
+        nc.vector.tensor_copy(out=picked[:, 0:S], in_=xs_t[:].indirect(offs_t[:]))
+        for r in range(4):
+            nc.sync.dma_start(out=planes[r:P:32, :].bitcast(I32), in_=picked[32 + 4 * r : 96 : 16, :].bitcast(I32))
+        load_weight("vin", offset=4096 - 64)
+        q_vca = prepare("vca", True)
+        load_weight("wfo", "grp_vca")
         nc.vector.tensor_copy(out=eg[:], in_=ew_t[:].bitcast(U32).indirect(tok_t[:]))
-        nc.vector.tensor_copy(out=esg[:], in_=es_t[:].indirect(tok_t[:]))
+        load_weight("vfo", offset=8192)
+        load_weight("wex", offset=12288)
         nc.vector.tensor_copy(out=xg[:], in_=xw_t[:].bitcast(U32).indirect(offs_t[:]))
-        nc.vector.tensor_copy(out=xsg[:], in_=xs_t[:].indirect(offs_t[:]))
-        g = gate("g", "vca", "wca", ACT.Tanh, True)
-        a = gate("a", "win", "vin", ACT.Sigmoid)
-        f = gate("f", "wfo", "vfo", ACT.Sigmoid)
-        b = gate("b", "wex", "vex", ACT.Sigmoid)
+        load_weight("vex", offset=26624)
+        q_wca = prepare("wca", True)
+        cell_t = [load_cell(0, "raw_wca"), load_cell(1, "grp_wca")]
+        g = gate("g", [q_vca, q_wca], ACT.Tanh)
+        a = gate("a", [prepare("win", True), prepare("vin", False)], ACT.Sigmoid)
+        f = gate("f", [prepare("wfo", True), prepare("vfo", False)], ACT.Sigmoid)
+        b = gate("b", [prepare("wex", True), prepare("vex", False)], ACT.Sigmoid)
         ag = []
         for m in range(M_TILES):
-            prod = raw[("vfo", "vex")[m]][:].rearrange("p j n -> p (j n)")[:, 0:S]
-            nc.vector.tensor_tensor(out=prod, in0=a[m][:], in1=g[m][:], op=ALU.mult)
+            prod = keep.tile([P, S], F32, name="ag%d" % m, tag=("grp_vfo", "grp_vex")[m], align_bytes=64)
+            nc.vector.tensor_tensor(out=prod[:], in0=a[m][:], in1=g[m][:], op=ALU.mult)
             ag.append(prod)
 
         def finish(m):
@@ -140,13 +156,13 @@ def tile_picked_zlstm_std_p_kernel(
                 cols = slice(c0, c0 + S // 2)
                 window = cell_t[m][:].indirect(offs_t[:, cols.start // 16 : cols.stop // 16])
                 nc.vector.tensor_tensor(out=kept[:, cols], in0=window, in1=f[m][:, cols], op=ALU.mult)
-            for c0 in range(0, S, PIECE):
-                cols = slice(c0, c0 + PIECE)
+            for c0, c1 in zip(EDGES, EDGES[1:]):
+                cols = slice(c0, c1)
                 nc.vector.tensor_tensor(out=new[:, cols], in0=kept[:, cols], in1=ag[m][:, cols], op=ALU.add)
                 nc.scalar.activation(out=squashed[:, cols], in_=new[:, cols], func=ACT.Tanh)
             stored = 0
-            for c0 in range(0, S, PIECE):
-                cols = slice(c0, c0 + PIECE)
+            for c0, c1 in zip(EDGES, EDGES[1:]):
+                cols = slice(c0, c1)
                 nc.vector.tensor_tensor(out=res[:, cols], in0=b[m][:, cols], in1=squashed[:, cols], op=ALU.mult)
                 if cols.stop in STORE_AT[m]:
                     nc.sync.dma_start(out=out[m * P : (m + 1) * P, stored : cols.stop], in_=res[:, stored : cols.stop])

@@ -50,14 +50,15 @@ def tile_picked_zlstm_std_p_kernel(
         nc.vector.memset(xs_t[:].bitcast(I32), 0)
         nc.vector.memset(planes[:].bitcast(I32), 0)
 
-        weights = {"win": win, "vin": vin, "wfo": wfo, "vfo": vfo, "wex": wex, "vex": vex, "wca": wca, "vca": vca}
+        weights = {"win": win, "vin": vin, "wfo": wfo, "vfo": vfo, "wex": wex, "vex0": vex[:, 0:P], "vex1": vex[:, P:N], "wca": wca, "vca": vca}
         raw = {}
 
         def load_weight(name, slot=None, offset=None):
+            width = weights[name].shape[1]
             if offset is None:
-                raw[name] = keep.tile([P, PACK, N], F32, name="raw_" + name, tag=slot or "raw_" + name, align_bytes=64)
+                raw[name] = keep.tile([P, PACK, width], F32, name="raw_" + name, tag=slot or "raw_" + name, align_bytes=64)
             else:
-                raw[name] = reuse.tile([P, PACK, N], F32, name="raw_" + name, align_bytes=64, offset=offset)
+                raw[name] = reuse.tile([P, PACK, width], F32, name="raw_" + name, align_bytes=64, offset=offset)
             nc.sync.dma_start(out=raw[name][:], in_=weights[name].rearrange("(p j) n -> p j n", j=PACK))
 
         def load_words(tile, words):
@@ -72,7 +73,7 @@ def tile_picked_zlstm_std_p_kernel(
             return tile
 
         def interleave(name, on_scalar):
-            grouped = keep.tile([P, N, PACK], BF16, name="grp_" + name, align_bytes=64)
+            grouped = keep.tile([P, weights[name].shape[1], PACK], BF16, name="grp_" + name, align_bytes=64)
             dst = grouped[:].rearrange("p (c i) t -> p c t i", i=4)
             src = raw[name][:].rearrange("p t (c i) -> p c t i", i=4)
             if on_scalar:
@@ -82,11 +83,12 @@ def tile_picked_zlstm_std_p_kernel(
             return grouped
 
         def quantise(name, grouped):
-            codes = keep.tile([P, N], U32, name="codes_" + name, align_bytes=64)
+            width = grouped.shape[1]
+            codes = keep.tile([P, width], U32, name="codes_" + name, align_bytes=64)
             if name in ("vca", "wca"):
                 scales = reuse.tile([P, N], U8, name="scales_" + name, align_bytes=64, offset=2560 + 256 * (name == "wca"))
             else:
-                scales = keep.tile([P, N], U8, name="scales_" + name, align_bytes=64)
+                scales = keep.tile([P, width], U8, name="scales_" + name, align_bytes=64)
             nc.vector.quantize_mx(
                 out=codes[:].bitcast(FP8X4), scales=scales[:], in_=grouped[:].rearrange("p c t -> p (c t)")
             )
@@ -100,7 +102,10 @@ def tile_picked_zlstm_std_p_kernel(
             for m in range(M_TILES):
                 rows = slice(m * P, (m + 1) * P)
                 acc = psum.tile([P, S], F32, name="acc_%s%d" % (name, m))
-                for i, (weight, side) in enumerate(terms):
+                for i, term in enumerate(terms):
+                    if isinstance(term, list):
+                        term, rows = term[m], slice(0, P)
+                    weight, side = term
                     nc.tensor.matmul_mx(
                         out=acc[:], lhsT=weight[0][:, rows].bitcast(FP8X4), lhsT_scale=weight[1][:, rows],
                         rhs=side[0].bitcast(FP8X4), rhs_scale=side[1], start=(i == 0), stop=(i == 1),
@@ -134,16 +139,19 @@ def tile_picked_zlstm_std_p_kernel(
         load_weight("vfo", offset=8192)
         load_weight("wex", offset=12288)
         nc.vector.tensor_copy(out=xg[:], in_=xw_t[:].bitcast(U32).indirect(offs_t[:]))
-        load_weight("vex", offset=26624)
+        load_weight("vex0", offset=26624)
         q_wca = prepare("wca", True)
-        cell_t = [load_cell(0, "raw_wca"), load_cell(1, "grp_wca")]
+        cell_t = [load_cell(0, "raw_wca")]
+        load_weight("vex1", "grp_wca")
+        q_win = prepare("win", True)
+        cell_t.append(load_cell(1, "raw_win"))
         g = gate("g", [q_vca, q_wca], ACT.Tanh)
-        a = gate("a", [prepare("win", True), prepare("vin", False)], ACT.Sigmoid)
+        a = gate("a", [q_win, prepare("vin", False)], ACT.Sigmoid)
         f = gate("f", [prepare("wfo", True), prepare("vfo", False)], ACT.Sigmoid)
-        b = gate("b", [prepare("wex", True), prepare("vex", False)], ACT.Sigmoid)
+        b = gate("b", [prepare("wex", True), [prepare("vex0", False), prepare("vex1", True)]], ACT.Sigmoid)
         ag = []
         for m in range(M_TILES):
-            prod = keep.tile([P, S], F32, name="ag%d" % m, tag=("grp_vfo", "grp_vex")[m], align_bytes=64)
+            prod = keep.tile([P, S], F32, name="ag%d" % m, tag=("grp_vfo", "grp_vex0")[m], align_bytes=64)
             nc.vector.tensor_tensor(out=prod[:], in0=a[m][:], in1=g[m][:], op=ALU.mult)
             ag.append(prod)
 

@@ -17,9 +17,25 @@ ALU = mybir.AluOpType
 
 P = 128
 PACK = 4
-M_TILES = N // P
-EDGES = (0, 128, 256, 384, 448, 512)
-STORE_AT = ((512,), (256, 512))
+UNIT_TILES = N // P
+PER_COLUMN = 16
+ALIGN = 64
+
+ROWS_FROM, ROWS_TO, ROWS_STEP = 32, 96, 4
+
+EDGES = (0, 128, 256, 384, 512)
+STORE_AT = ((S,), (S // 2, S))
+
+KIB = 1024
+XS_AT = 2 * KIB
+EG_AT = ALIGN
+VCA_SCALES_AT = XS_AT + KIB // 2
+VIN_AT = XS_AT + T - ALIGN
+EW_AT = 10 * KIB
+VFO_AT = EW_AT - 2 * KIB
+WEX_AT = EW_AT + 2 * KIB
+XW_AT = 20 * KIB
+VEX0_AT = XW_AT + 6 * KIB
 
 
 def tile_picked_zlstm_std_p_kernel(
@@ -31,49 +47,54 @@ def tile_picked_zlstm_std_p_kernel(
         reuse = ctx.enter_context(tc.tile_pool(name="reuse", bufs=1))
         psum = ctx.enter_context(tc.psum_pool(name="psum", bufs=1))
 
-        offs_t = keep.tile([P, S // 16], U16, name="offs_t")
-        tok_t = keep.tile([P, S // 16], U16, name="tok_t")
-        xw_t = reuse.tile([P, T], I32, name="xw_t", align_bytes=64, offset=20480)
-        ew_t = reuse.tile([P, W], I32, name="ew_t", align_bytes=64, offset=10240)
-        xs_t = reuse.tile([P, T], U8, name="xs_t", align_bytes=64, offset=2048)
+        offs_t = keep.tile([P, S // PER_COLUMN], U16, name="offs_t")
+        tok_t = keep.tile([P, S // PER_COLUMN], U16, name="tok_t")
+        xw_t = reuse.tile([P, T], I32, name="xw_t", align_bytes=ALIGN, offset=XW_AT)
+        ew_t = reuse.tile([P, W], I32, name="ew_t", align_bytes=ALIGN, offset=EW_AT)
+        xs_t = reuse.tile([P, T], U8, name="xs_t", align_bytes=ALIGN, offset=XS_AT)
         es_t = keep.tile([P, W], U8, name="es_t")
-        xg = keep.tile([P, S], U32, name="xg", align_bytes=64)
-        eg = reuse.tile([P, S], U32, name="eg", align_bytes=64, offset=64)
-        picked = keep.tile([P, 2 * S], U8, name="picked", align_bytes=64)
-        planes = keep.tile([P, 2 * S], U8, name="planes", align_bytes=64)
+        xg = keep.tile([P, S], U32, name="xg", align_bytes=ALIGN)
+        eg = reuse.tile([P, S], U32, name="eg", align_bytes=ALIGN, offset=EG_AT)
+        picked = keep.tile([P, 2 * S], U8, name="picked", align_bytes=ALIGN)
+        planes = keep.tile([P, 2 * S], U8, name="planes", align_bytes=ALIGN)
 
         warm = keep.tile([P, 1], F32, name="warm")
         warm_out = keep.tile([P, 1], F32, name="warm_out")
-        nc.gpsimd.memset(warm[:], 0.0)
+        nc.vector.memset(warm[:], 0.0)
         nc.scalar.activation(out=warm_out[:], in_=warm[:], func=ACT.Sigmoid)
         nc.vector.memset(es_t[:].bitcast(I32), 0)
         nc.vector.memset(xs_t[:].bitcast(I32), 0)
         nc.vector.memset(planes[:].bitcast(I32), 0)
 
-        weights = {"win": win, "vin": vin, "wfo": wfo, "vfo": vfo, "wex": wex, "vex0": vex[:, 0:P], "vex1": vex[:, P:N], "wca": wca, "vca": vca}
+        weights = {
+            "win": win, "vin": vin, "wfo": wfo, "vfo": vfo, "wex": wex,
+            "vex0": vex[:, 0:P], "vex1": vex[:, P:N], "wca": wca, "vca": vca,
+        }
         raw = {}
 
         def load_weight(name, slot=None, offset=None):
             width = weights[name].shape[1]
             if offset is None:
-                raw[name] = keep.tile([P, PACK, width], F32, name="raw_" + name, tag=slot or "raw_" + name, align_bytes=64)
+                raw[name] = keep.tile(
+                    [P, PACK, width], F32, name="raw_" + name, tag=slot or "raw_" + name, align_bytes=ALIGN
+                )
             else:
-                raw[name] = reuse.tile([P, PACK, width], F32, name="raw_" + name, align_bytes=64, offset=offset)
+                raw[name] = reuse.tile([P, PACK, width], F32, name="raw_" + name, align_bytes=ALIGN, offset=offset)
             nc.sync.dma_start(out=raw[name][:], in_=weights[name].rearrange("(p j) n -> p j n", j=PACK))
 
         def load_words(tile, words):
             nc.sync.dma_start(out=tile[:], in_=words[0].rearrange("p n t -> p (n t)").bitcast(I32))
 
         def load_scales(tile, scales):
-            nc.sync.dma_start(out=tile[32:96:4, :].bitcast(I32), in_=scales[0].bitcast(I32))
+            nc.sync.dma_start(out=tile[ROWS_FROM:ROWS_TO:ROWS_STEP, :].bitcast(I32), in_=scales[0].bitcast(I32))
 
         def load_cell(m, slot):
-            tile = keep.tile([P, T], F32, name="cell%d" % m, tag=slot, align_bytes=64)
+            tile = keep.tile([P, T], F32, name="cell%d" % m, tag=slot, align_bytes=ALIGN)
             nc.sync.dma_start(out=tile[:], in_=cell[m * P : (m + 1) * P, :])
             return tile
 
         def interleave(name, on_scalar):
-            grouped = keep.tile([P, weights[name].shape[1], PACK], BF16, name="grp_" + name, align_bytes=64)
+            grouped = keep.tile([P, weights[name].shape[1], PACK], BF16, name="grp_" + name, align_bytes=ALIGN)
             dst = grouped[:].rearrange("p (c i) t -> p c t i", i=4)
             src = raw[name][:].rearrange("p t (c i) -> p c t i", i=4)
             if on_scalar:
@@ -82,13 +103,13 @@ def tile_picked_zlstm_std_p_kernel(
                 nc.vector.tensor_copy(out=dst, in_=src)
             return grouped
 
-        def quantise(name, grouped):
+        def quantise(name, grouped, offset):
             width = grouped.shape[1]
-            codes = keep.tile([P, width], U32, name="codes_" + name, align_bytes=64)
-            if name in ("vca", "wca"):
-                scales = reuse.tile([P, N], U8, name="scales_" + name, align_bytes=64, offset=2560 + 256 * (name == "wca"))
+            codes = keep.tile([P, width], U32, name="codes_" + name, align_bytes=ALIGN)
+            if offset is None:
+                scales = keep.tile([P, width], U8, name="scales_" + name, align_bytes=ALIGN)
             else:
-                scales = keep.tile([P, width], U8, name="scales_" + name, align_bytes=64)
+                scales = reuse.tile([P, width], U8, name="scales_" + name, align_bytes=ALIGN, offset=offset)
             nc.vector.quantize_mx(
                 out=codes[:].bitcast(FP8X4), scales=scales[:], in_=grouped[:].rearrange("p c t -> p (c t)")
             )
@@ -97,26 +118,24 @@ def tile_picked_zlstm_std_p_kernel(
         x_side = (xg[:], planes[:, 0:S])
         e_side = (eg[:], planes[:, S : 2 * S])
 
-        def gate(name, terms, func):
+        def prepare(name, on_scalar, offset=None):
+            codes, scales = quantise(name, interleave(name, on_scalar), offset)
+            side = x_side if name[0] == "w" else e_side
+            return [(codes[:, c0 : c0 + P], scales[:, c0 : c0 + P], side) for c0 in range(0, codes.shape[1], P)]
+
+        def gate(name, first, second, func):
             tiles = []
-            for m in range(M_TILES):
-                rows = slice(m * P, (m + 1) * P)
+            for m in range(UNIT_TILES):
                 acc = psum.tile([P, S], F32, name="acc_%s%d" % (name, m))
-                for i, term in enumerate(terms):
-                    if isinstance(term, list):
-                        term, rows = term[m], slice(0, P)
-                    weight, side = term
+                for i, (codes, scales, side) in enumerate((first[m], second[m])):
                     nc.tensor.matmul_mx(
-                        out=acc[:], lhsT=weight[0][:, rows].bitcast(FP8X4), lhsT_scale=weight[1][:, rows],
+                        out=acc[:], lhsT=codes.bitcast(FP8X4), lhsT_scale=scales,
                         rhs=side[0].bitcast(FP8X4), rhs_scale=side[1], start=(i == 0), stop=(i == 1),
                     )
                 val = keep.tile([P, S], F32, name="%s%d" % (name, m))
                 nc.scalar.activation(out=val[:], in_=acc[:], func=func)
                 tiles.append(val)
             return tiles
-
-        def prepare(name, on_scalar):
-            return quantise(name, interleave(name, on_scalar)), x_side if name[0] == "w" else e_side
 
         load_weight("vca")
         nc.sync.dma_start(tok_t[:], tok)
@@ -131,38 +150,44 @@ def tile_picked_zlstm_std_p_kernel(
         nc.vector.tensor_copy(out=picked[:, S : 2 * S], in_=es_t[:].indirect(tok_t[:]))
         nc.vector.tensor_copy(out=picked[:, 0:S], in_=xs_t[:].indirect(offs_t[:]))
         for r in range(4):
-            nc.sync.dma_start(out=planes[r:P:32, :].bitcast(I32), in_=picked[32 + 4 * r : 96 : 16, :].bitcast(I32))
-        load_weight("vin", offset=4096 - 64)
-        q_vca = prepare("vca", True)
+            nc.sync.dma_start(
+                out=planes[r:P:32, :].bitcast(I32),
+                in_=picked[ROWS_FROM + ROWS_STEP * r : ROWS_TO : 4 * ROWS_STEP, :].bitcast(I32),
+            )
+
+        load_weight("vin", offset=VIN_AT)
+        q_vca = prepare("vca", True, VCA_SCALES_AT)
         load_weight("wfo", "grp_vca")
         nc.vector.tensor_copy(out=eg[:], in_=ew_t[:].bitcast(U32).indirect(tok_t[:]))
-        load_weight("vfo", offset=8192)
-        load_weight("wex", offset=12288)
+        load_weight("vfo", offset=VFO_AT)
+        load_weight("wex", offset=WEX_AT)
         nc.vector.tensor_copy(out=xg[:], in_=xw_t[:].bitcast(U32).indirect(offs_t[:]))
-        load_weight("vex0", offset=26624)
+        load_weight("vex0", offset=VEX0_AT)
         q_wca = prepare("wca", True)
         cell_t = [load_cell(0, "raw_wca")]
         load_weight("vex1", "grp_wca")
         q_win = prepare("win", True)
         cell_t.append(load_cell(1, "raw_win"))
-        g = gate("g", [q_vca, q_wca], ACT.Tanh)
-        a = gate("a", [q_win, prepare("vin", False)], ACT.Sigmoid)
-        f = gate("f", [prepare("wfo", True), prepare("vfo", False)], ACT.Sigmoid)
-        b = gate("b", [prepare("wex", True), [prepare("vex0", False), prepare("vex1", True)]], ACT.Sigmoid)
+
+        g = gate("g", q_vca, q_wca, ACT.Tanh)
+        a = gate("a", q_win, prepare("vin", False), ACT.Sigmoid)
+        f = gate("f", prepare("wfo", True), prepare("vfo", False), ACT.Sigmoid)
+        b = gate("b", prepare("wex", True), prepare("vex0", False) + prepare("vex1", True), ACT.Sigmoid)
+
         ag = []
-        for m in range(M_TILES):
-            prod = keep.tile([P, S], F32, name="ag%d" % m, tag=("grp_vfo", "grp_vex0")[m], align_bytes=64)
+        for m, slot in enumerate(("grp_vfo", "grp_vex0")):
+            prod = keep.tile([P, S], F32, name="ag%d" % m, tag=slot, align_bytes=ALIGN)
             nc.vector.tensor_tensor(out=prod[:], in0=a[m][:], in1=g[m][:], op=ALU.mult)
             ag.append(prod)
 
-        def finish(m):
+        for m in range(UNIT_TILES):
             kept = keep.tile([P, S], F32, name="kept%d" % m)
             new = keep.tile([P, S], F32, name="new%d" % m)
             squashed = keep.tile([P, S], F32, name="sq%d" % m)
             res = keep.tile([P, S], F32, name="res%d" % m)
             for c0 in range(0, S, S // 2):
                 cols = slice(c0, c0 + S // 2)
-                window = cell_t[m][:].indirect(offs_t[:, cols.start // 16 : cols.stop // 16])
+                window = cell_t[m][:].indirect(offs_t[:, cols.start // PER_COLUMN : cols.stop // PER_COLUMN])
                 nc.vector.tensor_tensor(out=kept[:, cols], in0=window, in1=f[m][:, cols], op=ALU.mult)
             for c0, c1 in zip(EDGES, EDGES[1:]):
                 cols = slice(c0, c1)
@@ -172,9 +197,6 @@ def tile_picked_zlstm_std_p_kernel(
             for c0, c1 in zip(EDGES, EDGES[1:]):
                 cols = slice(c0, c1)
                 nc.vector.tensor_tensor(out=res[:, cols], in0=b[m][:, cols], in1=squashed[:, cols], op=ALU.mult)
-                if cols.stop in STORE_AT[m]:
-                    nc.sync.dma_start(out=out[m * P : (m + 1) * P, stored : cols.stop], in_=res[:, stored : cols.stop])
-                    stored = cols.stop
-
-        for m in range(M_TILES):
-            finish(m)
+                if c1 in STORE_AT[m]:
+                    nc.sync.dma_start(out=out[m * P : (m + 1) * P, stored:c1], in_=res[:, stored:c1])
+                    stored = c1

@@ -19,7 +19,7 @@ P = 128
 PACK = 4
 UNIT_TILES = N // P
 PER_COLUMN = 16
-ALIGN = 64
+ALIGN = 256
 
 ROWS_FROM, ROWS_TO, ROWS_STEP = 32, 96, 4
 
@@ -52,7 +52,7 @@ def tile_picked_zlstm_std_p_kernel(
         xw_t = reuse.tile([P, T], I32, name="xw_t", align_bytes=ALIGN, offset=XW_AT)
         ew_t = reuse.tile([P, W], I32, name="ew_t", align_bytes=ALIGN, offset=EW_AT)
         xs_t = reuse.tile([P, T], U8, name="xs_t", align_bytes=ALIGN, offset=XS_AT)
-        es_t = keep.tile([P, W], U8, name="es_t")
+        es_t = keep.tile([P, W], U8, name="es_t", align_bytes=ALIGN)
         xg = keep.tile([P, S], U32, name="xg", align_bytes=ALIGN)
         eg = reuse.tile([P, S], U32, name="eg", align_bytes=ALIGN, offset=EG_AT)
         picked = keep.tile([P, 2 * S], U8, name="picked", align_bytes=ALIGN)
@@ -184,7 +184,7 @@ def tile_picked_zlstm_std_p_kernel(
             kept = keep.tile([P, S], F32, name="kept%d" % m)
             new = keep.tile([P, S], F32, name="new%d" % m)
             squashed = keep.tile([P, S], F32, name="sq%d" % m)
-            res = keep.tile([P, S], F32, name="res%d" % m)
+            res = keep.tile([P, S], F32, name="res%d" % m, align_bytes=ALIGN)
             for c0 in range(0, S, S // 2):
                 cols = slice(c0, c0 + S // 2)
                 window = cell_t[m][:].indirect(offs_t[:, cols.start // PER_COLUMN : cols.stop // PER_COLUMN])

@@ -19,7 +19,7 @@ P = 128
 PACK = 4
 UNIT_TILES = N // P
 PER_COLUMN = 16
-ALIGN = 256
+ALIGN = 512
 
 ROWS_FROM, ROWS_TO, ROWS_STEP = 32, 96, 4
 
@@ -95,8 +95,9 @@ def tile_picked_zlstm_std_p_kernel(
 
         def interleave(name, on_scalar):
             grouped = keep.tile([P, weights[name].shape[1], PACK], BF16, name="grp_" + name, align_bytes=ALIGN)
-            dst = grouped[:].rearrange("p (c i) t -> p c t i", i=4)
-            src = raw[name][:].rearrange("p t (c i) -> p c t i", i=4)
+            run = 2 if on_scalar else 4
+            dst = grouped[:].rearrange("p (c i) t -> p c t i", i=run)
+            src = raw[name][:].rearrange("p t (c i) -> p c t i", i=run)
             if on_scalar:
                 nc.scalar.copy(out=dst, in_=src)
             else:

from contextlib import ExitStack

import concourse.mybir as mybir

K, T, S, W, N = 512, 2048, 512, 1024, 256
FLOPS = 8 * 2 * K * N * S

F32 = mybir.dt.float32
BF16 = mybir.dt.bfloat16
I32 = mybir.dt.int32
U32 = mybir.dt.uint32
U16 = mybir.dt.uint16
U8 = mybir.dt.uint8
FP8X4 = mybir.dt.float8_e4m3fn_x4
ACT = mybir.ActivationFunctionType
ALU = mybir.AluOpType

P = 128
PACK = 4
UNIT_TILES = N // P
PER_COLUMN = 16
ALIGN = 512

ROWS_FROM, ROWS_TO, ROWS_STEP = 32, 96, 4

EDGES = (0, 128, 256, 384, 512)
STORE_AT = ((S,), (S // 2, S))

KIB = 1024
XS_AT = 2 * KIB
EG_AT = ALIGN
VCA_SCALES_AT = XS_AT + KIB // 2
VIN_AT = XS_AT + T - ALIGN
EW_AT = 10 * KIB
VFO_AT = EW_AT - 2 * KIB
WEX_AT = EW_AT + 2 * KIB
XW_AT = 20 * KIB
VEX0_AT = XW_AT + 6 * KIB


def tile_picked_zlstm_std_p_kernel(
    tc, x_words, x_scales, e_words, e_scales, win, vin, wfo, vfo, wex, vex, wca, vca, cell, offs, tok, out
):
    nc = tc.nc
    with ExitStack() as ctx:
        keep = ctx.enter_context(tc.tile_pool(name="keep", bufs=1))
        reuse = ctx.enter_context(tc.tile_pool(name="reuse", bufs=1))
        psum = ctx.enter_context(tc.psum_pool(name="psum", bufs=1))

        offs_t = keep.tile([P, S // PER_COLUMN], U16, name="offs_t")
        tok_t = keep.tile([P, S // PER_COLUMN], U16, name="tok_t")
        xw_t = reuse.tile([P, T], I32, name="xw_t", align_bytes=ALIGN, offset=XW_AT)
        ew_t = reuse.tile([P, W], I32, name="ew_t", align_bytes=ALIGN, offset=EW_AT)
        xs_t = reuse.tile([P, T], U8, name="xs_t", align_bytes=ALIGN, offset=XS_AT)
        es_t = keep.tile([P, W], U8, name="es_t", align_bytes=ALIGN)
        xg = keep.tile([P, S], U32, name="xg", align_bytes=ALIGN)
        eg = reuse.tile([P, S], U32, name="eg", align_bytes=ALIGN, offset=EG_AT)
        picked = keep.tile([P, 2 * S], U8, name="picked", align_bytes=ALIGN)
        planes = keep.tile([P, 2 * S], U8, name="planes", align_bytes=ALIGN)

        warm = keep.tile([P, 1], F32, name="warm")
        warm_out = keep.tile([P, 1], F32, name="warm_out")
        nc.vector.memset(warm[:], 0.0)
        nc.scalar.activation(out=warm_out[:], in_=warm[:], func=ACT.Sigmoid)
        nc.vector.memset(es_t[:].bitcast(I32), 0)
        nc.vector.memset(xs_t[:].bitcast(I32), 0)
        nc.vector.memset(planes[:].bitcast(I32), 0)

        weights = {
            "win": win, "vin": vin, "wfo": wfo, "vfo": vfo, "wex": wex,
            "vex0": vex[:, 0:P], "vex1": vex[:, P:N], "wca": wca, "vca": vca,
        }
        raw = {}

        def load_weight(name, slot=None, offset=None):
            width = weights[name].shape[1]
            if offset is None:
                raw[name] = keep.tile(
                    [P, PACK, width], F32, name="raw_" + name, tag=slot or "raw_" + name, align_bytes=ALIGN
                )
            else:
                raw[name] = reuse.tile([P, PACK, width], F32, name="raw_" + name, align_bytes=ALIGN, offset=offset)
            nc.sync.dma_start(out=raw[name][:], in_=weights[name].rearrange("(p j) n -> p j n", j=PACK))

        def load_words(tile, words):
            nc.sync.dma_start(out=tile[:], in_=words[0].rearrange("p n t -> p (n t)").bitcast(I32))

        def load_scales(tile, scales):
            nc.sync.dma_start(out=tile[ROWS_FROM:ROWS_TO:ROWS_STEP, :].bitcast(I32), in_=scales[0].bitcast(I32))

        def load_cell(m, slot):
            tile = keep.tile([P, T], F32, name="cell%d" % m, tag=slot, align_bytes=ALIGN)
            nc.sync.dma_start(out=tile[:], in_=cell[m * P : (m + 1) * P, :])
            return tile

        def interleave(name, on_scalar):
            grouped = keep.tile([P, weights[name].shape[1], PACK], BF16, name="grp_" + name, align_bytes=ALIGN)
            run = 2 if on_scalar else 4
            dst = grouped[:].rearrange("p (c i) t -> p c t i", i=run)
            src = raw[name][:].rearrange("p t (c i) -> p c t i", i=run)
            if on_scalar:
                nc.scalar.copy(out=dst, in_=src)
            else:
                nc.vector.tensor_copy(out=dst, in_=src)
            return grouped

        def quantise(name, grouped, offset):
            width = grouped.shape[1]
            codes = keep.tile([P, width], U32, name="codes_" + name, align_bytes=ALIGN)
            if offset is None:
                scales = keep.tile([P, width], U8, name="scales_" + name, align_bytes=ALIGN)
            else:
                scales = reuse.tile([P, width], U8, name="scales_" + name, align_bytes=ALIGN, offset=offset)
            nc.vector.quantize_mx(
                out=codes[:].bitcast(FP8X4), scales=scales[:], in_=grouped[:].rearrange("p c t -> p (c t)")
            )
            return codes, scales

        x_side = (xg[:], planes[:, 0:S])
        e_side = (eg[:], planes[:, S : 2 * S])

        def prepare(name, on_scalar, offset=None):
            codes, scales = quantise(name, interleave(name, on_scalar), offset)
            side = x_side if name[0] == "w" else e_side
            return [(codes[:, c0 : c0 + P], scales[:, c0 : c0 + P], side) for c0 in range(0, codes.shape[1], P)]

        def gate(name, first, second, func):
            tiles = []
            for m in range(UNIT_TILES):
                acc = psum.tile([P, S], F32, name="acc_%s%d" % (name, m))
                for i, (codes, scales, side) in enumerate((first[m], second[m])):
                    nc.tensor.matmul_mx(
                        out=acc[:], lhsT=codes.bitcast(FP8X4), lhsT_scale=scales,
                        rhs=side[0].bitcast(FP8X4), rhs_scale=side[1], start=(i == 0), stop=(i == 1),
                    )
                val = keep.tile([P, S], F32, name="%s%d" % (name, m))
                nc.scalar.activation(out=val[:], in_=acc[:], func=func)
                tiles.append(val)
            return tiles

        load_weight("vca")
        nc.sync.dma_start(tok_t[:], tok)
        nc.sync.dma_start(offs_t[:], offs)
        load_scales(es_t, e_scales)
        load_words(ew_t, e_words)
        load_scales(xs_t, x_scales)
        load_words(xw_t, x_words)
        load_weight("wca")
        load_weight("win")

        nc.vector.tensor_copy(out=picked[:, S : 2 * S], in_=es_t[:].indirect(tok_t[:]))
        nc.vector.tensor_copy(out=picked[:, 0:S], in_=xs_t[:].indirect(offs_t[:]))
        for r in range(4):
            nc.sync.dma_start(
                out=planes[r:P:32, :].bitcast(I32),
                in_=picked[ROWS_FROM + ROWS_STEP * r : ROWS_TO : 4 * ROWS_STEP, :].bitcast(I32),
            )

        load_weight("vin", offset=VIN_AT)
        q_vca = prepare("vca", True, VCA_SCALES_AT)
        load_weight("wfo", "grp_vca")
        nc.vector.tensor_copy(out=eg[:], in_=ew_t[:].bitcast(U32).indirect(tok_t[:]))
        load_weight("vfo", offset=VFO_AT)
        load_weight("wex", offset=WEX_AT)
        nc.vector.tensor_copy(out=xg[:], in_=xw_t[:].bitcast(U32).indirect(offs_t[:]))
        load_weight("vex0", offset=VEX0_AT)
        q_wca = prepare("wca", True)
        cell_t = [load_cell(0, "raw_wca")]
        load_weight("vex1", "grp_wca")
        q_win = prepare("win", True)
        cell_t.append(load_cell(1, "raw_win"))

        g = gate("g", q_vca, q_wca, ACT.Tanh)
        a = gate("a", q_win, prepare("vin", False), ACT.Sigmoid)
        f = gate("f", prepare("wfo", True), prepare("vfo", False), ACT.Sigmoid)
        b = gate("b", prepare("wex", True), prepare("vex0", False) + prepare("vex1", True), ACT.Sigmoid)

        ag = []
        for m, slot in enumerate(("grp_vfo", "grp_vex0")):
            prod = keep.tile([P, S], F32, name="ag%d" % m, tag=slot, align_bytes=ALIGN)
            nc.vector.tensor_tensor(out=prod[:], in0=a[m][:], in1=g[m][:], op=ALU.mult)
            ag.append(prod)

        for m in range(UNIT_TILES):
            kept = keep.tile([P, S], F32, name="kept%d" % m)
            new = keep.tile([P, S], F32, name="new%d" % m)
            squashed = keep.tile([P, S], F32, name="sq%d" % m)
            res = keep.tile([P, S], F32, name="res%d" % m, align_bytes=ALIGN)
            for c0 in range(0, S, S // 2):
                cols = slice(c0, c0 + S // 2)
                window = cell_t[m][:].indirect(offs_t[:, cols.start // PER_COLUMN : cols.stop // PER_COLUMN])
                nc.vector.tensor_tensor(out=kept[:, cols], in0=window, in1=f[m][:, cols], op=ALU.mult)
            for c0, c1 in zip(EDGES, EDGES[1:]):
                cols = slice(c0, c1)
                nc.vector.tensor_tensor(out=new[:, cols], in0=kept[:, cols], in1=ag[m][:, cols], op=ALU.add)
                nc.scalar.activation(out=squashed[:, cols], in_=new[:, cols], func=ACT.Tanh)
            stored = 0
            for c0, c1 in zip(EDGES, EDGES[1:]):
                cols = slice(c0, c1)
                nc.vector.tensor_tensor(out=res[:, cols], in0=b[m][:, cols], in1=squashed[:, cols], op=ALU.mult)
                if c1 in STORE_AT[m]:
                    nc.sync.dma_start(out=out[m * P : (m + 1) * P, stored:c1], in_=res[:, stored:c1])
                    stored = c1
